import numpy as np
import ml_dtypes


def mxq(x, axis, fmt="e4m3"):
    dtype, down = {"e4m3": (ml_dtypes.float8_e4m3fn, 7), "e5m2": (ml_dtypes.float8_e5m2, 14)}[fmt]
    v = np.moveaxis(np.asarray(x, np.float32).astype(ml_dtypes.bfloat16).astype(np.float64), axis, -1)
    blocks = v.reshape(v.shape[:-1] + (-1, 32))
    amax = np.abs(blocks).max(-1, keepdims=True)
    byte = np.maximum(np.where(amax > 0, np.frexp(amax)[1] - 1 + 127, 0) - down, 1)
    scale = np.exp2(byte - 127.0)
    codes = (blocks / scale).astype(np.float32).astype(dtype).astype(np.float64)
    return np.moveaxis((codes * scale).reshape(v.shape), -1, axis)


WIDE = False


def mx_kscale(k):
    if not WIDE:
        return np.ones(k)
    levels = np.array([10, -10, 5, -5, 0])
    if k % 512:
        return np.exp2(np.random.permutation(np.resize(levels, k // 32))).repeat(32)
    a = np.empty((k // 512, 16))
    for p in range(k // 512):
        a[p, :8] = np.random.permutation(np.resize(levels, 8))
        for g in range(8):
            far = levels[np.abs(levels - a[p, g]) >= 10]
            a[p, g + 8] = far[np.random.randint(len(far))]
    return np.exp2(a.ravel()).repeat(32)


def f64(x):
    return np.asarray(x).astype(np.float64)


def striped8(idx):
    return np.asarray(idx).reshape(8, -1, 16).transpose(0, 2, 1).reshape(128, -1).astype(np.uint16)


def unstriped8(offs):
    return offs.reshape(8, 16, -1).transpose(0, 2, 1).reshape(8, -1).astype(np.int64)


def pick8(x, idx, run):
    r = np.arange(len(x))
    return x[r[:, None], idx[r % (8 * run) // run]]


E2M1 = np.array([0.0, 0.5, 1.0, 1.5, 2.0, 3.0, 4.0, 6.0, -0.0, -0.5, -1.0, -1.5, -2.0, -3.0, -4.0, -6.0])


def pack_weight(w, fmt):
    k, n = w.shape
    w = f64(np.asarray(w, np.float32).astype(ml_dtypes.bfloat16)).reshape(k // 32, 32, n)
    amax = np.abs(w).max(1)
    if fmt == "e4m3":
        byte = np.frexp(amax)[1] - 1 + 127 - 7
    else:
        mant, ex = np.frexp(amax / 6.0)
        byte = np.where(mant > 0.5, ex, ex - 1) + 127
    byte = np.clip(np.where(amax > 0, byte, 1), 1, 254)
    scaled = (w * np.exp2(127.0 - byte)[:, None, :]).reshape(k, n).astype(np.float32)
    by_word = np.ascontiguousarray(scaled.reshape(k // 512, 128, 4, n).transpose(0, 1, 3, 2))
    if fmt == "e4m3":
        words = by_word.astype(ml_dtypes.float8_e4m3fn).view(np.uint8)
    else:
        c = by_word.astype(ml_dtypes.float4_e2m1fn).view(np.uint8) & 0xF
        words = (c[..., 0::2] | (c[..., 1::2] << 4)).reshape(k // 512, 128, 2 * n)
    return np.ascontiguousarray(words), np.ascontiguousarray(byte.astype(np.uint8).reshape(k // 512, 16, n))


def unpack_weight(words, scales, fmt):
    g, _, n = scales.shape
    words = np.ascontiguousarray(words).reshape(g, 128, n, -1)
    if fmt == "e4m3":
        vals = words.view(ml_dtypes.float8_e4m3fn).astype(np.float64)
    else:
        nib = np.empty((g, 128, n, 4), np.uint8)
        nib[..., 0::2] = words & 0xF
        nib[..., 1::2] = words >> 4
        vals = E2M1[nib]
    vals = vals * np.repeat(np.exp2(scales.astype(np.float64) - 127.0), 8, axis=1)[..., None]
    return vals.transpose(0, 1, 3, 2).reshape(g * 512, n)


def sigmoid(v):
    return 1.0 / (1.0 + np.exp(-v))


D, T, I, Q = 512, 1024, 512, 128


def setup_inputs():
    n = np.random.standard_normal
    idx = np.stack([np.random.permutation(T)[:I] for _ in range(8)])
    idx2 = np.stack([np.random.permutation(T)[:I] for _ in range(8)])
    idx3 = np.stack([np.random.permutation(T)[:I] for _ in range(8)])
    fd = mx_kscale(D)
    keysp = pack_weight(n((D, T)) / fd[:, None], "e4m3")
    return {
        "query": (n((D, Q)) * 1.0 / np.sqrt(D) * fd[:, None]).astype(np.float32),
        "keys_words": keysp[0],
        "keys_scales": keysp[1],
        "lam": (np.random.uniform(0.3, 0.9, (Q, 1))).astype(np.float32),
        "eager": (np.random.uniform(0.8, 2.0, (Q, 1))).astype(np.float32),
        "thresh": (np.random.uniform(1.5, 4.0, (Q, 1))).astype(np.float32),
        "base": (0.3 * n((Q, I))).astype(np.float32),
        "gain2": (np.random.uniform(0.5, 2.0, (Q, 1))).astype(np.float32),
        "offs": striped8(idx),
        "offs2": striped8(idx2),
        "offs3": striped8(idx3),
    }


def reference(query, keys_words, keys_scales, lam, eager, thresh, base, gain2, offs, offs2, offs3):
    idx = unstriped8(offs)
    idx2 = unstriped8(offs2)
    idx3 = unstriped8(offs3)
    keysu = unpack_weight(keys_words, keys_scales, "e4m3")
    queryq = mxq(f64(query), 0, "e4m3")
    a = queryq.T @ keysu
    rv = np.log(np.exp(pick8(a, idx2, 16)) + np.exp(pick8(a, idx3, 16)))
    s = pick8(a, idx, 16) - rv * f64(lam)
    m0 = np.max(s, axis=1, keepdims=True)
    m1 = np.mean(s, axis=1, keepdims=True)
    p = np.exp(s - m0)
    gt0 = sigmoid((m0 - m1) * f64(eager) - f64(thresh))
    w = p / np.sum(p, axis=1, keepdims=True) * gt0
    y = np.tanh(w * f64(gain2) * 256.0) + f64(base)
    return y

@@ -1,0 +1,170 @@
+import math
+from contextlib import ExitStack
+
+import concourse.mybir as mybir
+
+F32 = mybir.dt.float32
+BF16 = mybir.dt.bfloat16
+I32 = mybir.dt.int32
+U32 = mybir.dt.uint32
+U16 = mybir.dt.uint16
+U8 = mybir.dt.uint8
+FP8X4 = mybir.dt.float8_e4m3fn_x4
+ALU = mybir.AluOpType
+ACT = mybir.ActivationFunctionType
+AXIS = mybir.AxisListType
+
+P = 128
+D, T, I, Q = 512, 1024, 512, 128
+PACK = 4
+CHUNKS = 4
+N = T // CHUNKS
+HALF = I // 2
+CAP = 24.0
+
+FLOPS = 2 * D * Q * T
+
+
+def tile_attend_tworivals_abstaining_gated_heads_kernel(
+    tc, query, keys_words, keys_scales, lam, eager, thresh, base, gain2, offs, offs2, offs3, out
+):
+    nc = tc.nc
+    with ExitStack() as ctx:
+        sb = ctx.enter_context(tc.tile_pool(name="sb", bufs=1))
+        ps = ctx.enter_context(tc.psum_pool(name="ps", bufs=1))
+
+        q_raw = sb.tile([P, PACK, Q], F32, name="q_raw")
+        k_words = [sb.tile([P, T // 2], U32, name=f"k_words{h}", align_bytes=64) for h in range(2)]
+        k_scales = sb.tile([P, N], U8, name="k_scales", align_bytes=64)
+        own_list = sb.tile([P, I // 16], U16, name="own_list")
+        rival2_list = sb.tile([P, I // 16], U16, name="rival2_list")
+        rival3_list = sb.tile([P, I // 16], U16, name="rival3_list")
+        lam_c = sb.tile([P, 1], F32, name="lam_c")
+        eager_c = sb.tile([P, 1], F32, name="eager_c")
+        thresh_c = sb.tile([P, 1], F32, name="thresh_c")
+        gain_c = sb.tile([P, 1], F32, name="gain_c")
+        base_t = sb.tile([P, I], F32, name="base_t")
+
+        nc.vector.memset(k_scales[:].bitcast(I32), 0)
+        nc.sync.dma_start(out=q_raw[:], in_=query.rearrange("(p j) q -> p j q", j=PACK))
+        k_dram = keys_words[0].rearrange("p n t -> p (n t)").bitcast(I32)
+        for h in range(2):
+            nc.sync.dma_start(out=k_words[h][:].bitcast(I32), in_=k_dram[:, h * (T // 2) : (h + 1) * (T // 2)])
+        for quad in range(4):
+            nc.scalar.dma_start(
+                out=k_scales[32 * quad : 32 * quad + 16, :].bitcast(I32),
+                in_=keys_scales[0, 4 * quad : 4 * quad + 4, :]
+                .bitcast(I32)
+                .rearrange("r (c w) -> c r w", c=CHUNKS),
+            )
+        nc.sync.dma_start(rival3_list[:], offs3)
+        nc.sync.dma_start(rival2_list[:], offs2)
+        nc.sync.dma_start(own_list[:], offs)
+        nc.sync.dma_start(out=lam_c[:], in_=lam)
+        nc.sync.dma_start(out=eager_c[:], in_=eager)
+        nc.sync.dma_start(out=thresh_c[:], in_=thresh)
+        nc.sync.dma_start(out=gain_c[:], in_=gain2)
+        nc.sync.dma_start(out=base_t[:], in_=base)
+
+        q_bf = sb.tile([P, Q, PACK], BF16, name="q_bf", align_bytes=64)
+        nc.vector.tensor_copy(
+            out=q_bf[:].rearrange("p (c i) j -> p c j i", i=4),
+            in_=q_raw[:].rearrange("p j (c i) -> p c j i", i=4),
+        )
+        q_words = sb.tile([P, Q], U32, name="q_words", align_bytes=64)
+        q_scales = sb.tile([P, Q], U8, name="q_scales", align_bytes=64)
+        nc.vector.quantize_mx(
+            out=q_words[:].bitcast(FP8X4),
+            scales=q_scales[:],
+            in_=q_bf[:].rearrange("p q j -> p (q j)"),
+        )
+
+        a = sb.tile([P, T], F32, name="a")
+        for c in range(CHUNKS):
+            cols = slice(c * N, (c + 1) * N)
+            bank = ps.tile([P, N], F32, name=f"bank{c}")
+            nc.tensor.matmul_mx(
+                out=bank[:],
+                lhsT=q_words[:].bitcast(FP8X4),
+                lhsT_scale=q_scales[:],
+                rhs=k_words[c // 2][:, (c % 2) * N : (c % 2 + 1) * N].bitcast(FP8X4),
+                rhs_scale=k_scales[4 * c : P, :],
+                start=True,
+                stop=True,
+            )
+            if c % 2 == 0:
+                nc.scalar.copy(out=a[:, cols], in_=bank[:])
+            else:
+                nc.vector.tensor_copy(out=a[:, cols], in_=bank[:])
+
+        neg_half_eager = sb.tile([P, 1], F32, name="neg_half_eager")
+        nc.gpsimd.tensor_scalar(neg_half_eager[:], eager_c[:], -0.5, 0.0, ALU.mult, ALU.add)
+        eager_mean = sb.tile([P, 1], F32, name="eager_mean")
+        nc.gpsimd.tensor_scalar(eager_mean[:], eager_c[:], 0.5 / I, 0.0, ALU.mult, ALU.add)
+        half_thresh = sb.tile([P, 1], F32, name="half_thresh")
+        nc.gpsimd.tensor_scalar(half_thresh[:], thresh_c[:], 0.5, 0.0, ALU.mult, ALU.add)
+
+        cols_a, cols_b = slice(0, HALF), slice(HALF, I)
+        list_a, list_b = slice(0, HALF // 16), slice(HALF // 16, I // 16)
+        a3 = sb.tile([P, I], F32, name="a3")
+        a1_a = sb.tile([P, HALF], F32, name="a1_a")
+        gap = sb.tile([P, I], F32, name="gap")
+        e_gap = sb.tile([P, I], F32, name="e_gap")
+        nc.scalar.activation(a3[:, cols_a], a[:].indirect(rival3_list[:, list_a]), ACT.Copy)
+        nc.vector.tensor_copy(a3[:, cols_b], a[:].indirect(rival3_list[:, list_b]))
+        nc.scalar.activation(a1_a[:], a[:].indirect(own_list[:, list_a]), ACT.Copy)
+        for cols, entries in ((cols_b, list_b), (cols_a, list_a)):
+            nc.vector.tensor_tensor(gap[:, cols], a[:].indirect(rival2_list[:, entries]), a3[:, cols], ALU.subtract)
+            nc.scalar.activation(e_gap[:, cols], gap[:, cols], ACT.Exp)
+
+        lead = sb.tile([P, I], F32, name="lead")
+        nc.vector.scalar_tensor_tensor(lead[:], gap[:], CAP, a3[:], ALU.max, ALU.add)
+        one_plus = sb.tile([P, I], F32, name="one_plus")
+        nc.vector.tensor_scalar(one_plus[:], e_gap[:], math.exp(CAP), 1.0, ALU.min, ALU.add)
+        soft = sb.tile([P, I], F32, name="soft")
+        for cols in (cols_a, cols_b):
+            nc.scalar.activation(soft[:, cols], one_plus[:, cols], ACT.Ln)
+
+        lam_lead_b = sb.tile([P, HALF], F32, name="lam_lead_b")
+        nc.vector.tensor_scalar(lam_lead_b[:], lead[:, cols_b], lam_c[:], None, ALU.mult)
+        rest_a = sb.tile([P, HALF], F32, name="rest_a")
+        nc.vector.scalar_tensor_tensor(rest_a[:], lead[:, cols_a], lam_c[:], a1_a[:], ALU.mult, ALU.subtract)
+        neg_rest_b = sb.tile([P, HALF], F32, name="neg_rest_b")
+        nc.vector.tensor_tensor(neg_rest_b[:], a[:].indirect(own_list[:, list_b]), lam_lead_b[:], ALU.subtract)
+
+        neg_s = sb.tile([P, I], F32, name="neg_s")
+        neg_sum_a = sb.tile([P, 1], F32, name="neg_sum_a")
+        neg_sum_b = sb.tile([P, 1], F32, name="neg_sum_b")
+        nc.vector.scalar_tensor_tensor(
+            neg_s[:, cols_a], soft[:, cols_a], lam_c[:], rest_a[:], ALU.mult, ALU.add, accum_out=neg_sum_a[:]
+        )
+        nc.vector.scalar_tensor_tensor(
+            neg_s[:, cols_b], soft[:, cols_b], lam_c[:], neg_rest_b[:], ALU.mult, ALU.subtract, accum_out=neg_sum_b[:]
+        )
+        bias_a = sb.tile([P, 1], F32, name="bias_a")
+        nc.vector.tensor_scalar(bias_a[:], neg_sum_a[:], eager_mean[:], half_thresh[:], ALU.mult, ALU.subtract)
+        gate_bias = sb.tile([P, 1], F32, name="gate_bias")
+        nc.vector.tensor_scalar(gate_bias[:], neg_sum_b[:], eager_mean[:], bias_a[:], ALU.mult, ALU.add)
+        neg_m0 = sb.tile([P, 1], F32, name="neg_m0")
+        nc.vector.tensor_reduce(neg_m0[:], neg_s[:], AXIS.X, ALU.min)
+
+        half_tanh = sb.tile([P, 1], F32, name="half_tanh")
+        nc.scalar.activation(half_tanh[:], neg_m0[:], ACT.Tanh, bias=gate_bias[:], scale=neg_half_eager[:])
+        p = sb.tile([P, I], F32, name="p")
+        p_sum = sb.tile([P, 1], F32, name="p_sum")
+        nc.scalar.activation(p[:], neg_s[:], ACT.Exp, bias=neg_m0[:], scale=-1.0, accum_out=p_sum[:])
+
+        gate_gain = sb.tile([P, 1], F32, name="gate_gain")
+        nc.vector.tensor_scalar(gate_gain[:], half_tanh[:], 1.0, gain_c[:], ALU.add, ALU.mult)
+        inv_sum = sb.tile([P, 1], F32, name="inv_sum")
+        nc.vector.reciprocal(inv_sum[:], p_sum[:])
+
+        gated = [sb.tile([P, HALF], F32, name=f"gated{h}") for h in range(2)]
+        for h, cols in enumerate((cols_a, cols_b)):
+            nc.vector.tensor_scalar(gated[h][:], p[:, cols], gate_gain[:], 128.0, ALU.mult, ALU.mult)
+        for h, cols in enumerate((cols_a, cols_b)):
+            bent = sb.tile([P, HALF], F32, name=f"bent{h}")
+            nc.scalar.activation(bent[:], gated[h][:], ACT.Tanh, scale=inv_sum[:])
+            y = sb.tile([P, HALF], F32, name=f"y{h}")
+            nc.vector.tensor_tensor(y[:], bent[:], base_t[:, cols], ALU.add)
+            nc.sync.dma_start(out=out[:, cols], in_=y[:])

@@ -21,6 +21,8 @@ CHUNKS = 4
 N = T // CHUNKS
 HALF = I // 2
 CAP = 24.0
+PASS_WIDTHS = (256, 256, 256, 128, 128)
+OUT_WIDTHS = (128, 256, 128)
 
 FLOPS = 2 * D * Q * T
 
@@ -47,16 +49,16 @@ def tile_attend_tworivals_abstaining_gated_heads_kernel(
 
         nc.vector.memset(k_scales[:].bitcast(I32), 0)
         nc.sync.dma_start(out=q_raw[:], in_=query.rearrange("(p j) q -> p j q", j=PACK))
-        k_dram = keys_words[0].rearrange("p n t -> p (n t)").bitcast(I32)
-        for h in range(2):
-            nc.sync.dma_start(out=k_words[h][:].bitcast(I32), in_=k_dram[:, h * (T // 2) : (h + 1) * (T // 2)])
         for quad in range(4):
-            nc.scalar.dma_start(
+            nc.sync.dma_start(
                 out=k_scales[32 * quad : 32 * quad + 16, :].bitcast(I32),
                 in_=keys_scales[0, 4 * quad : 4 * quad + 4, :]
                 .bitcast(I32)
                 .rearrange("r (c w) -> c r w", c=CHUNKS),
             )
+        k_dram = keys_words[0].rearrange("p n t -> p (n t)").bitcast(I32)
+        for h in range(2):
+            nc.sync.dma_start(out=k_words[h][:].bitcast(I32), in_=k_dram[:, h * (T // 2) : (h + 1) * (T // 2)])
         nc.sync.dma_start(rival3_list[:], offs3)
         nc.sync.dma_start(rival2_list[:], offs2)
         nc.sync.dma_start(own_list[:], offs)
@@ -80,41 +82,39 @@ def tile_attend_tworivals_abstaining_gated_heads_kernel(
         )
 
         a = sb.tile([P, T], F32, name="a")
-        for c in range(CHUNKS):
-            cols = slice(c * N, (c + 1) * N)
-            bank = ps.tile([P, N], F32, name=f"bank{c}")
+        start = 0
+        for n, width in enumerate(PASS_WIDTHS):
+            cols = slice(start, start + width)
+            plane, first = divmod(start, N)
+            bank = ps.tile([P, width], F32, name=f"bank{n}")
             nc.tensor.matmul_mx(
                 out=bank[:],
                 lhsT=q_words[:].bitcast(FP8X4),
                 lhsT_scale=q_scales[:],
-                rhs=k_words[c // 2][:, (c % 2) * N : (c % 2 + 1) * N].bitcast(FP8X4),
-                rhs_scale=k_scales[4 * c : P, :],
+                rhs=k_words[start // (T // 2)][:, start % (T // 2) : start % (T // 2) + width].bitcast(FP8X4),
+                rhs_scale=k_scales[4 * plane : P, first : first + width],
                 start=True,
                 stop=True,
             )
-            if c % 2 == 0:
-                nc.scalar.copy(out=a[:, cols], in_=bank[:])
-            else:
+            if n % 2 == 0:
                 nc.vector.tensor_copy(out=a[:, cols], in_=bank[:])
-
-        neg_half_eager = sb.tile([P, 1], F32, name="neg_half_eager")
-        nc.gpsimd.tensor_scalar(neg_half_eager[:], eager_c[:], -0.5, 0.0, ALU.mult, ALU.add)
-        eager_mean = sb.tile([P, 1], F32, name="eager_mean")
-        nc.gpsimd.tensor_scalar(eager_mean[:], eager_c[:], 0.5 / I, 0.0, ALU.mult, ALU.add)
-        half_thresh = sb.tile([P, 1], F32, name="half_thresh")
-        nc.gpsimd.tensor_scalar(half_thresh[:], thresh_c[:], 0.5, 0.0, ALU.mult, ALU.add)
+            else:
+                nc.scalar.copy(out=a[:, cols], in_=bank[:])
+            start = start + width
 
         cols_a, cols_b = slice(0, HALF), slice(HALF, I)
         list_a, list_b = slice(0, HALF // 16), slice(HALF // 16, I // 16)
         a3 = sb.tile([P, I], F32, name="a3")
-        a1_a = sb.tile([P, HALF], F32, name="a1_a")
+        a2_a = sb.tile([P, HALF], F32, name="a2_a")
         gap = sb.tile([P, I], F32, name="gap")
         e_gap = sb.tile([P, I], F32, name="e_gap")
         nc.scalar.activation(a3[:, cols_a], a[:].indirect(rival3_list[:, list_a]), ACT.Copy)
+        nc.scalar.activation(a2_a[:], a[:].indirect(rival2_list[:, list_a]), ACT.Copy)
         nc.vector.tensor_copy(a3[:, cols_b], a[:].indirect(rival3_list[:, list_b]))
-        nc.scalar.activation(a1_a[:], a[:].indirect(own_list[:, list_a]), ACT.Copy)
-        for cols, entries in ((cols_b, list_b), (cols_a, list_a)):
-            nc.vector.tensor_tensor(gap[:, cols], a[:].indirect(rival2_list[:, entries]), a3[:, cols], ALU.subtract)
+        nc.vector.tensor_tensor(gap[:, cols_b], a[:].indirect(rival2_list[:, list_b]), a3[:, cols_b], ALU.subtract)
+        nc.scalar.activation(e_gap[:, cols_b], gap[:, cols_b], ACT.Exp)
+        for cols in (slice(0, HALF // 2), slice(HALF // 2, HALF)):
+            nc.vector.tensor_tensor(gap[:, cols], a2_a[:, cols], a3[:, cols], ALU.subtract)
             nc.scalar.activation(e_gap[:, cols], gap[:, cols], ACT.Exp)
 
         lead = sb.tile([P, I], F32, name="lead")
@@ -125,46 +125,49 @@ def tile_attend_tworivals_abstaining_gated_heads_kernel(
         for cols in (cols_a, cols_b):
             nc.scalar.activation(soft[:, cols], one_plus[:, cols], ACT.Ln)
 
-        lam_lead_b = sb.tile([P, HALF], F32, name="lam_lead_b")
-        nc.vector.tensor_scalar(lam_lead_b[:], lead[:, cols_b], lam_c[:], None, ALU.mult)
-        rest_a = sb.tile([P, HALF], F32, name="rest_a")
-        nc.vector.scalar_tensor_tensor(rest_a[:], lead[:, cols_a], lam_c[:], a1_a[:], ALU.mult, ALU.subtract)
-        neg_rest_b = sb.tile([P, HALF], F32, name="neg_rest_b")
-        nc.vector.tensor_tensor(neg_rest_b[:], a[:].indirect(own_list[:, list_b]), lam_lead_b[:], ALU.subtract)
+        lam_lead = sb.tile([P, I], F32, name="lam_lead")
+        nc.vector.tensor_scalar(lam_lead[:], lead[:], CAP, lam_c[:], ALU.subtract, ALU.mult)
+        own_less_lead = sb.tile([P, I], F32, name="own_less_lead")
+        for cols, entries in ((cols_a, list_a), (cols_b, list_b)):
+            nc.vector.tensor_tensor(
+                own_less_lead[:, cols], a[:].indirect(own_list[:, entries]), lam_lead[:, cols], ALU.subtract
+            )
 
         neg_s = sb.tile([P, I], F32, name="neg_s")
         neg_sum_a = sb.tile([P, 1], F32, name="neg_sum_a")
         neg_sum_b = sb.tile([P, 1], F32, name="neg_sum_b")
-        nc.vector.scalar_tensor_tensor(
-            neg_s[:, cols_a], soft[:, cols_a], lam_c[:], rest_a[:], ALU.mult, ALU.add, accum_out=neg_sum_a[:]
-        )
-        nc.vector.scalar_tensor_tensor(
-            neg_s[:, cols_b], soft[:, cols_b], lam_c[:], neg_rest_b[:], ALU.mult, ALU.subtract, accum_out=neg_sum_b[:]
-        )
-        bias_a = sb.tile([P, 1], F32, name="bias_a")
-        nc.vector.tensor_scalar(bias_a[:], neg_sum_a[:], eager_mean[:], half_thresh[:], ALU.mult, ALU.subtract)
-        gate_bias = sb.tile([P, 1], F32, name="gate_bias")
-        nc.vector.tensor_scalar(gate_bias[:], neg_sum_b[:], eager_mean[:], bias_a[:], ALU.mult, ALU.add)
+        for cols, neg_sum in ((cols_a, neg_sum_a), (cols_b, neg_sum_b)):
+            nc.vector.scalar_tensor_tensor(
+                neg_s[:, cols], soft[:, cols], lam_c[:], own_less_lead[:, cols], ALU.mult, ALU.subtract,
+                accum_out=neg_sum[:],
+            )
+        mean_s = sb.tile([P, 1], F32, name="mean_s")
+        nc.vector.tensor_scalar(mean_s[:], neg_sum_a[:], neg_sum_b[:], -1.0 / I, ALU.add, ALU.mult)
         neg_m0 = sb.tile([P, 1], F32, name="neg_m0")
         nc.vector.tensor_reduce(neg_m0[:], neg_s[:], AXIS.X, ALU.min)
+        gate_bias = sb.tile([P, 1], F32, name="gate_bias")
+        nc.vector.tensor_scalar(gate_bias[:], mean_s[:], eager_c[:], thresh_c[:], ALU.mult, ALU.add)
 
-        half_tanh = sb.tile([P, 1], F32, name="half_tanh")
-        nc.scalar.activation(half_tanh[:], neg_m0[:], ACT.Tanh, bias=gate_bias[:], scale=neg_half_eager[:])
+        odds = sb.tile([P, 1], F32, name="odds")
+        nc.scalar.activation(odds[:], neg_m0[:], ACT.Exp, bias=gate_bias[:], scale=eager_c[:])
         p = sb.tile([P, I], F32, name="p")
         p_sum = sb.tile([P, 1], F32, name="p_sum")
         nc.scalar.activation(p[:], neg_s[:], ACT.Exp, bias=neg_m0[:], scale=-1.0, accum_out=p_sum[:])
 
-        gate_gain = sb.tile([P, 1], F32, name="gate_gain")
-        nc.vector.tensor_scalar(gate_gain[:], half_tanh[:], 1.0, gain_c[:], ALU.add, ALU.mult)
+        inv_gate = sb.tile([P, 1], F32, name="inv_gate")
+        nc.vector.tensor_scalar(inv_gate[:], odds[:], 1.0, 1.0 / 256.0, ALU.add, ALU.mult)
+        gate256 = sb.tile([P, 1], F32, name="gate256")
+        nc.vector.reciprocal(gate256[:], inv_gate[:])
         inv_sum = sb.tile([P, 1], F32, name="inv_sum")
         nc.vector.reciprocal(inv_sum[:], p_sum[:])
 
-        gated = [sb.tile([P, HALF], F32, name=f"gated{h}") for h in range(2)]
-        for h, cols in enumerate((cols_a, cols_b)):
-            nc.vector.tensor_scalar(gated[h][:], p[:, cols], gate_gain[:], 128.0, ALU.mult, ALU.mult)
-        for h, cols in enumerate((cols_a, cols_b)):
-            bent = sb.tile([P, HALF], F32, name=f"bent{h}")
-            nc.scalar.activation(bent[:], gated[h][:], ACT.Tanh, scale=inv_sum[:])
-            y = sb.tile([P, HALF], F32, name=f"y{h}")
-            nc.vector.tensor_tensor(y[:], bent[:], base_t[:, cols], ALU.add)
-            nc.sync.dma_start(out=out[:, cols], in_=y[:])
+        pieces = [slice(sum(OUT_WIDTHS[:n]), sum(OUT_WIDTHS[: n + 1])) for n in range(len(OUT_WIDTHS))]
+        gated = sb.tile([P, I], F32, name="gated")
+        for cols in pieces:
+            nc.vector.tensor_scalar(gated[:, cols], p[:, cols], gate256[:], gain_c[:], ALU.mult, ALU.mult)
+        bent = sb.tile([P, I], F32, name="bent")
+        y = sb.tile([P, I], F32, name="y")
+        for cols in pieces:
+            nc.scalar.activation(bent[:, cols], gated[:, cols], ACT.Tanh, scale=inv_sum[:])
+            nc.vector.tensor_tensor(y[:, cols], bent[:, cols], base_t[:, cols], ALU.add)
+            nc.sync.dma_start(out=out[:, cols], in_=y[:, cols])

@@ -22,7 +22,9 @@ N = T // CHUNKS
 HALF = I // 2
 CAP = 24.0
 PASS_WIDTHS = (256, 256, 256, 128, 128)
-OUT_WIDTHS = (128, 256, 128)
+OUT_WIDTHS = (128, 128, 128, 128)
+CAST_SPLIT = 80
+LOAD_WIDTHS = (256, 512, 256)
 
 FLOPS = 2 * D * Q * T
 
@@ -36,7 +38,7 @@ def tile_attend_tworivals_abstaining_gated_heads_kernel(
         ps = ctx.enter_context(tc.psum_pool(name="ps", bufs=1))
 
         q_raw = sb.tile([P, PACK, Q], F32, name="q_raw")
-        k_words = [sb.tile([P, T // 2], U32, name=f"k_words{h}", align_bytes=64) for h in range(2)]
+        k_words = [sb.tile([P, w], U32, name=f"k_words{n}", align_bytes=64) for n, w in enumerate(LOAD_WIDTHS)]
         k_scales = sb.tile([P, N], U8, name="k_scales", align_bytes=64)
         own_list = sb.tile([P, I // 16], U16, name="own_list")
         rival2_list = sb.tile([P, I // 16], U16, name="rival2_list")
@@ -49,6 +51,13 @@ def tile_attend_tworivals_abstaining_gated_heads_kernel(
 
         nc.vector.memset(k_scales[:].bitcast(I32), 0)
         nc.sync.dma_start(out=q_raw[:], in_=query.rearrange("(p j) q -> p j q", j=PACK))
+        k_dram = keys_words[0].rearrange("p n t -> p (n t)").bitcast(I32)
+
+        def load_keys(n):
+            first = sum(LOAD_WIDTHS[:n])
+            nc.sync.dma_start(out=k_words[n][:].bitcast(I32), in_=k_dram[:, first : first + LOAD_WIDTHS[n]])
+
+        load_keys(0)
         for quad in range(4):
             nc.sync.dma_start(
                 out=k_scales[32 * quad : 32 * quad + 16, :].bitcast(I32),
@@ -56,9 +65,8 @@ def tile_attend_tworivals_abstaining_gated_heads_kernel(
                 .bitcast(I32)
                 .rearrange("r (c w) -> c r w", c=CHUNKS),
             )
-        k_dram = keys_words[0].rearrange("p n t -> p (n t)").bitcast(I32)
-        for h in range(2):
-            nc.sync.dma_start(out=k_words[h][:].bitcast(I32), in_=k_dram[:, h * (T // 2) : (h + 1) * (T // 2)])
+        load_keys(1)
+        load_keys(2)
         nc.sync.dma_start(rival3_list[:], offs3)
         nc.sync.dma_start(rival2_list[:], offs2)
         nc.sync.dma_start(own_list[:], offs)
@@ -70,8 +78,12 @@ def tile_attend_tworivals_abstaining_gated_heads_kernel(
 
         q_bf = sb.tile([P, Q, PACK], BF16, name="q_bf", align_bytes=64)
         nc.vector.tensor_copy(
-            out=q_bf[:].rearrange("p (c i) j -> p c j i", i=4),
-            in_=q_raw[:].rearrange("p j (c i) -> p c j i", i=4),
+            out=q_bf[:, 0:CAST_SPLIT, :].rearrange("p (c i) j -> p c j i", i=4),
+            in_=q_raw[:, :, 0:CAST_SPLIT].rearrange("p j (c i) -> p c j i", i=4),
+        )
+        nc.scalar.copy(
+            out=q_bf[:, CAST_SPLIT:Q, :].rearrange("p (c i) j -> p c j i", i=4),
+            in_=q_raw[:, :, CAST_SPLIT:Q].rearrange("p j (c i) -> p c j i", i=4),
         )
         q_words = sb.tile([P, Q], U32, name="q_words", align_bytes=64)
         q_scales = sb.tile([P, Q], U8, name="q_scales", align_bytes=64)
@@ -86,12 +98,14 @@ def tile_attend_tworivals_abstaining_gated_heads_kernel(
         for n, width in enumerate(PASS_WIDTHS):
             cols = slice(start, start + width)
             plane, first = divmod(start, N)
+            load = max(m for m in range(len(LOAD_WIDTHS)) if sum(LOAD_WIDTHS[:m]) <= start)
+            offset = start - sum(LOAD_WIDTHS[:load])
             bank = ps.tile([P, width], F32, name=f"bank{n}")
             nc.tensor.matmul_mx(
                 out=bank[:],
                 lhsT=q_words[:].bitcast(FP8X4),
                 lhsT_scale=q_scales[:],
-                rhs=k_words[start // (T // 2)][:, start % (T // 2) : start % (T // 2) + width].bitcast(FP8X4),
+                rhs=k_words[load][:, offset : offset + width].bitcast(FP8X4),
                 rhs_scale=k_scales[4 * plane : P, first : first + width],
                 start=True,
                 stop=True,
@@ -101,6 +115,9 @@ def tile_attend_tworivals_abstaining_gated_heads_kernel(
             else:
                 nc.scalar.copy(out=a[:, cols], in_=bank[:])
             start = start + width
+
+        neg_eager_mean = sb.tile([P, 1], F32, name="neg_eager_mean")
+        nc.gpsimd.tensor_scalar(neg_eager_mean[:], eager_c[:], -1.0 / I, 0.0, ALU.mult, ALU.add)
 
         cols_a, cols_b = slice(0, HALF), slice(HALF, I)
         list_a, list_b = slice(0, HALF // 16), slice(HALF // 16, I // 16)
@@ -141,12 +158,12 @@ def tile_attend_tworivals_abstaining_gated_heads_kernel(
                 neg_s[:, cols], soft[:, cols], lam_c[:], own_less_lead[:, cols], ALU.mult, ALU.subtract,
                 accum_out=neg_sum[:],
             )
-        mean_s = sb.tile([P, 1], F32, name="mean_s")
-        nc.vector.tensor_scalar(mean_s[:], neg_sum_a[:], neg_sum_b[:], -1.0 / I, ALU.add, ALU.mult)
-        neg_m0 = sb.tile([P, 1], F32, name="neg_m0")
-        nc.vector.tensor_reduce(neg_m0[:], neg_s[:], AXIS.X, ALU.min)
+        bias_a = sb.tile([P, 1], F32, name="bias_a")
+        nc.vector.tensor_scalar(bias_a[:], neg_sum_a[:], neg_eager_mean[:], thresh_c[:], ALU.mult, ALU.add)
         gate_bias = sb.tile([P, 1], F32, name="gate_bias")
-        nc.vector.tensor_scalar(gate_bias[:], mean_s[:], eager_c[:], thresh_c[:], ALU.mult, ALU.add)
+        nc.vector.tensor_scalar(gate_bias[:], neg_sum_b[:], neg_eager_mean[:], bias_a[:], ALU.mult, ALU.add)
+        neg_m0 = neg_sum_b
+        nc.vector.tensor_reduce(neg_m0[:], neg_s[:], AXIS.X, ALU.min)
 
         odds = sb.tile([P, 1], F32, name="odds")
         nc.scalar.activation(odds[:], neg_m0[:], ACT.Exp, bias=gate_bias[:], scale=eager_c[:])

@@ -22,8 +22,7 @@ N = T // CHUNKS
 HALF = I // 2
 CAP = 24.0
 PASS_WIDTHS = (256, 256, 256, 128, 128)
-OUT_WIDTHS = (128, 128, 128, 128)
-CAST_SPLIT = 80
+OUT_WIDTHS = (128, 256, 128)
 LOAD_WIDTHS = (256, 512, 256)
 
 FLOPS = 2 * D * Q * T
@@ -78,12 +77,8 @@ def tile_attend_tworivals_abstaining_gated_heads_kernel(
 
         q_bf = sb.tile([P, Q, PACK], BF16, name="q_bf", align_bytes=64)
         nc.vector.tensor_copy(
-            out=q_bf[:, 0:CAST_SPLIT, :].rearrange("p (c i) j -> p c j i", i=4),
-            in_=q_raw[:, :, 0:CAST_SPLIT].rearrange("p j (c i) -> p c j i", i=4),
-        )
-        nc.scalar.copy(
-            out=q_bf[:, CAST_SPLIT:Q, :].rearrange("p (c i) j -> p c j i", i=4),
-            in_=q_raw[:, :, CAST_SPLIT:Q].rearrange("p j (c i) -> p c j i", i=4),
+            out=q_bf[:].rearrange("p (c i) j -> p c j i", i=4),
+            in_=q_raw[:].rearrange("p j (c i) -> p c j i", i=4),
         )
         q_words = sb.tile([P, Q], U32, name="q_words", align_bytes=64)
         q_scales = sb.tile([P, Q], U8, name="q_scales", align_bytes=64)

import math
from contextlib import ExitStack

import concourse.mybir as mybir

F32 = mybir.dt.float32
BF16 = mybir.dt.bfloat16
I32 = mybir.dt.int32
U32 = mybir.dt.uint32
U16 = mybir.dt.uint16
U8 = mybir.dt.uint8
FP8X4 = mybir.dt.float8_e4m3fn_x4
ALU = mybir.AluOpType
ACT = mybir.ActivationFunctionType
AXIS = mybir.AxisListType

P = 128
D, T, I, Q = 512, 1024, 512, 128
PACK = 4
CHUNKS = 4
N = T // CHUNKS
HALF = I // 2
CAP = 24.0
PASS_WIDTHS = (256, 256, 256, 128, 128)
OUT_WIDTHS = (128, 256, 128)
LOAD_WIDTHS = (256, 512, 256)

FLOPS = 2 * D * Q * T


def tile_attend_tworivals_abstaining_gated_heads_kernel(
    tc, query, keys_words, keys_scales, lam, eager, thresh, base, gain2, offs, offs2, offs3, out
):
    nc = tc.nc
    with ExitStack() as ctx:
        sb = ctx.enter_context(tc.tile_pool(name="sb", bufs=1))
        ps = ctx.enter_context(tc.psum_pool(name="ps", bufs=1))

        q_raw = sb.tile([P, PACK, Q], F32, name="q_raw")
        k_words = [sb.tile([P, w], U32, name=f"k_words{n}", align_bytes=64) for n, w in enumerate(LOAD_WIDTHS)]
        k_scales = sb.tile([P, N], U8, name="k_scales", align_bytes=64)
        own_list = sb.tile([P, I // 16], U16, name="own_list")
        rival2_list = sb.tile([P, I // 16], U16, name="rival2_list")
        rival3_list = sb.tile([P, I // 16], U16, name="rival3_list")
        lam_c = sb.tile([P, 1], F32, name="lam_c")
        eager_c = sb.tile([P, 1], F32, name="eager_c")
        thresh_c = sb.tile([P, 1], F32, name="thresh_c")
        gain_c = sb.tile([P, 1], F32, name="gain_c")
        base_t = sb.tile([P, I], F32, name="base_t")

        nc.vector.memset(k_scales[:].bitcast(I32), 0)
        nc.sync.dma_start(out=q_raw[:], in_=query.rearrange("(p j) q -> p j q", j=PACK))
        k_dram = keys_words[0].rearrange("p n t -> p (n t)").bitcast(I32)

        def load_keys(n):
            first = sum(LOAD_WIDTHS[:n])
            nc.sync.dma_start(out=k_words[n][:].bitcast(I32), in_=k_dram[:, first : first + LOAD_WIDTHS[n]])

        load_keys(0)
        for quad in range(4):
            nc.sync.dma_start(
                out=k_scales[32 * quad : 32 * quad + 16, :].bitcast(I32),
                in_=keys_scales[0, 4 * quad : 4 * quad + 4, :]
                .bitcast(I32)
                .rearrange("r (c w) -> c r w", c=CHUNKS),
            )
        load_keys(1)
        load_keys(2)
        nc.sync.dma_start(rival3_list[:], offs3)
        nc.sync.dma_start(rival2_list[:], offs2)
        nc.sync.dma_start(own_list[:], offs)
        nc.sync.dma_start(out=lam_c[:], in_=lam)
        nc.sync.dma_start(out=eager_c[:], in_=eager)
        nc.sync.dma_start(out=thresh_c[:], in_=thresh)
        nc.sync.dma_start(out=gain_c[:], in_=gain2)
        nc.sync.dma_start(out=base_t[:], in_=base)

        q_bf = sb.tile([P, Q, PACK], BF16, name="q_bf", align_bytes=64)
        nc.vector.tensor_copy(
            out=q_bf[:].rearrange("p (c i) j -> p c j i", i=4),
            in_=q_raw[:].rearrange("p j (c i) -> p c j i", i=4),
        )
        q_words = sb.tile([P, Q], U32, name="q_words", align_bytes=64)
        q_scales = sb.tile([P, Q], U8, name="q_scales", align_bytes=64)
        nc.vector.quantize_mx(
            out=q_words[:].bitcast(FP8X4),
            scales=q_scales[:],
            in_=q_bf[:].rearrange("p q j -> p (q j)"),
        )

        a = sb.tile([P, T], F32, name="a")
        start = 0
        for n, width in enumerate(PASS_WIDTHS):
            cols = slice(start, start + width)
            plane, first = divmod(start, N)
            load = max(m for m in range(len(LOAD_WIDTHS)) if sum(LOAD_WIDTHS[:m]) <= start)
            offset = start - sum(LOAD_WIDTHS[:load])
            bank = ps.tile([P, width], F32, name=f"bank{n}")
            nc.tensor.matmul_mx(
                out=bank[:],
                lhsT=q_words[:].bitcast(FP8X4),
                lhsT_scale=q_scales[:],
                rhs=k_words[load][:, offset : offset + width].bitcast(FP8X4),
                rhs_scale=k_scales[4 * plane : P, first : first + width],
                start=True,
                stop=True,
            )
            if n % 2 == 0:
                nc.vector.tensor_copy(out=a[:, cols], in_=bank[:])
            else:
                nc.scalar.copy(out=a[:, cols], in_=bank[:])
            start = start + width

        neg_eager_mean = sb.tile([P, 1], F32, name="neg_eager_mean")
        nc.gpsimd.tensor_scalar(neg_eager_mean[:], eager_c[:], -1.0 / I, 0.0, ALU.mult, ALU.add)

        cols_a, cols_b = slice(0, HALF), slice(HALF, I)
        list_a, list_b = slice(0, HALF // 16), slice(HALF // 16, I // 16)
        a3 = sb.tile([P, I], F32, name="a3")
        a2_a = sb.tile([P, HALF], F32, name="a2_a")
        gap = sb.tile([P, I], F32, name="gap")
        e_gap = sb.tile([P, I], F32, name="e_gap")
        nc.scalar.activation(a3[:, cols_a], a[:].indirect(rival3_list[:, list_a]), ACT.Copy)
        nc.scalar.activation(a2_a[:], a[:].indirect(rival2_list[:, list_a]), ACT.Copy)
        nc.vector.tensor_copy(a3[:, cols_b], a[:].indirect(rival3_list[:, list_b]))
        nc.vector.tensor_tensor(gap[:, cols_b], a[:].indirect(rival2_list[:, list_b]), a3[:, cols_b], ALU.subtract)
        nc.scalar.activation(e_gap[:, cols_b], gap[:, cols_b], ACT.Exp)
        for cols in (slice(0, HALF // 2), slice(HALF // 2, HALF)):
            nc.vector.tensor_tensor(gap[:, cols], a2_a[:, cols], a3[:, cols], ALU.subtract)
            nc.scalar.activation(e_gap[:, cols], gap[:, cols], ACT.Exp)

        lead = sb.tile([P, I], F32, name="lead")
        nc.vector.scalar_tensor_tensor(lead[:], gap[:], CAP, a3[:], ALU.max, ALU.add)
        one_plus = sb.tile([P, I], F32, name="one_plus")
        nc.vector.tensor_scalar(one_plus[:], e_gap[:], math.exp(CAP), 1.0, ALU.min, ALU.add)
        soft = sb.tile([P, I], F32, name="soft")
        for cols in (cols_a, cols_b):
            nc.scalar.activation(soft[:, cols], one_plus[:, cols], ACT.Ln)

        lam_lead = sb.tile([P, I], F32, name="lam_lead")
        nc.vector.tensor_scalar(lam_lead[:], lead[:], CAP, lam_c[:], ALU.subtract, ALU.mult)
        own_less_lead = sb.tile([P, I], F32, name="own_less_lead")
        for cols, entries in ((cols_a, list_a), (cols_b, list_b)):
            nc.vector.tensor_tensor(
                own_less_lead[:, cols], a[:].indirect(own_list[:, entries]), lam_lead[:, cols], ALU.subtract
            )

        neg_s = sb.tile([P, I], F32, name="neg_s")
        neg_sum_a = sb.tile([P, 1], F32, name="neg_sum_a")
        neg_sum_b = sb.tile([P, 1], F32, name="neg_sum_b")
        for cols, neg_sum in ((cols_a, neg_sum_a), (cols_b, neg_sum_b)):
            nc.vector.scalar_tensor_tensor(
                neg_s[:, cols], soft[:, cols], lam_c[:], own_less_lead[:, cols], ALU.mult, ALU.subtract,
                accum_out=neg_sum[:],
            )
        bias_a = sb.tile([P, 1], F32, name="bias_a")
        nc.vector.tensor_scalar(bias_a[:], neg_sum_a[:], neg_eager_mean[:], thresh_c[:], ALU.mult, ALU.add)
        gate_bias = sb.tile([P, 1], F32, name="gate_bias")
        nc.vector.tensor_scalar(gate_bias[:], neg_sum_b[:], neg_eager_mean[:], bias_a[:], ALU.mult, ALU.add)
        neg_m0 = neg_sum_b
        nc.vector.tensor_reduce(neg_m0[:], neg_s[:], AXIS.X, ALU.min)

        odds = sb.tile([P, 1], F32, name="odds")
        nc.scalar.activation(odds[:], neg_m0[:], ACT.Exp, bias=gate_bias[:], scale=eager_c[:])
        p = sb.tile([P, I], F32, name="p")
        p_sum = sb.tile([P, 1], F32, name="p_sum")
        nc.scalar.activation(p[:], neg_s[:], ACT.Exp, bias=neg_m0[:], scale=-1.0, accum_out=p_sum[:])

        inv_gate = sb.tile([P, 1], F32, name="inv_gate")
        nc.vector.tensor_scalar(inv_gate[:], odds[:], 1.0, 1.0 / 256.0, ALU.add, ALU.mult)
        gate256 = sb.tile([P, 1], F32, name="gate256")
        nc.vector.reciprocal(gate256[:], inv_gate[:])
        inv_sum = sb.tile([P, 1], F32, name="inv_sum")
        nc.vector.reciprocal(inv_sum[:], p_sum[:])

        pieces = [slice(sum(OUT_WIDTHS[:n]), sum(OUT_WIDTHS[: n + 1])) for n in range(len(OUT_WIDTHS))]
        gated = sb.tile([P, I], F32, name="gated")
        for cols in pieces:
            nc.vector.tensor_scalar(gated[:, cols], p[:, cols], gate256[:], gain_c[:], ALU.mult, ALU.mult)
        bent = sb.tile([P, I], F32, name="bent")
        y = sb.tile([P, I], F32, name="y")
        for cols in pieces:
            nc.scalar.activation(bent[:, cols], gated[:, cols], ACT.Tanh, scale=inv_sum[:])
            nc.vector.tensor_tensor(y[:, cols], bent[:, cols], base_t[:, cols], ALU.add)
            nc.sync.dma_start(out=out[:, cols], in_=y[:, cols])
